import numpy as np, ml_dtypes
CORES = [25,29,65,69,153,157,193,197]
N = 8
import mx_ref
NC = 128
BF = ml_dtypes.bfloat16
def setup_inputs(rng):
    def f(*shape):
        return mx_ref.flush((rng.standard_normal(shape, dtype=np.float32) * np.exp2(rng.integers(-2, 3, shape[:-1] + (1,)))).astype(BF))
    return {"w": f(N, 128, 512), "x": f(N, 128, N * 4 * NC)}
def setup_inputs_blocks(rng):
    d = setup_inputs(rng)
    for k in ("w", "x"): d[k] = mx_ref.spread(d[k], rng, 2)
    return d
def setup_inputs_wide(rng):
    d = setup_inputs(rng)
    for k in ("w", "x"): d[k] = mx_ref.flush((d[k].astype(np.float32) * np.exp2(rng.integers(-8, 9, (N, 1, 1))).astype(np.float32)).astype(BF))
    return d
def setup_inputs_zeros(rng):
    d = setup_inputs(rng); v = d["x"].reshape(N, 128, -1, 4).copy()
    v[np.broadcast_to((rng.random((N, 1, v.shape[2], 1)) < 0.33), v.shape)] = 0
    d["x"] = v.reshape(d["x"].shape)
    return d
def reference(w, x):
    QW = [mx_ref.quantize(w[j]) for j in range(N)]
    y = np.zeros((N, 128, NC), np.float32)
    for r in range(N):
        for j in range(N):
            p = mx_ref.matmul(QW[j], mx_ref.quantize(x[j][:, 4 * NC * r:4 * NC * r + 4 * NC]))
            y[r] = p if j == 0 else y[r] + p
    return {"y": y}

from concourse.bass import DstId, RemoteDMATransfer
from concourse.mybir import dt

N = 8
C = 128
E = 4 * C

SCRATCH = {
    "wt": ("sbuf", [128, E], "bfloat16"),
    "xt": ("sbuf", [128, N * E], "bfloat16"),
    "q": ("sbuf", [128, (N + 1) * C], "float8_e4m3fn_x4"),
    "s": ("sbuf", [128, (N + 1) * C], "uint8"),
    "lq": ("sbuf", [128, 2 * N * C], "float8_e4m3fn_x4"),
    "ls": ("sbuf", [128, 2 * N * C], "uint8"),
    "o": ("sbuf", [128, C], "float32"),
    "ps": ("psum", [128, 512], "float32"),
}
GROUPS = ["A1", "A2", "B", "P", "O"]
SEMAPHORES = (["lW", "qW"] + ["l" + k for k in GROUPS] + ["q" + k for k in GROUPS] + ["a%d" % j for j in range(N)]
              + ["b%d" % j for j in range(N)] + ["rwc", "rws", "rxc", "rxs", "sent", "mm", "cp", "st"])
CODES, PLANE = 0, 1


def _bits(m):
    return [e for e in range(m.bit_length()) if (m >> e) & 1]


def _split(es, n):
    k = len(es) // n
    return [es[i * k:(i + 1) * k] for i in range(n)]


def _plan(cores, topo):
    world = range((max(topo.host(c) for c in cores) + 1) * topo.CORES_PER_HOST)
    rank = {c: i for i, c in enumerate(cores)}

    def here(a, b):
        return topo.host(a) == topo.host(b) and topo.chip(a) == topo.chip(b)

    sets = {}
    for c in cores:
        peer = [d for d in cores if d != c and here(c, d)]
        plane = [d for d in cores if topo.same_plane(c, d)]
        cross = [d for d in cores if d != c and d not in peer and d not in plane]
        sets[c] = {"peer": peer, "plane": plane, "cross": cross,
                   "near": [d for d in cross if topo.host(d) == topo.host(c)],
                   "far": [d for d in cross if topo.host(d) != topo.host(c)]}
    wslot = {c: i for i, c in enumerate(sorted(cores, key=lambda c: (topo.chip(c), topo.die(c), topo.host(c))))}

    calls, expect, need = {}, {}, {}

    def add(core, kind, gates, trs, srcs=()):
        calls.setdefault(core, []).append((gates, kind, trs))
        for t in trs:
            expect[(t[0], t[6])] = expect.get((t[0], t[6]), 0) + len(t[5])
            for j in srcs:
                need.setdefault((t[0], j), set()).add(t[6])

    def owners(c, pair):
        return [k for k in world if k not in rank and topo.mates(k, pair[0]) and topo.die(k) == topo.die(c)
                and topo.may_write(c, k) and all(topo.may_write(k, d) for d in pair)]

    def engines(src, on_chip, off_chip):
        on, off = _bits(topo.mask(src, on_chip)), _bits(topo.mask(src, off_chip))
        return off, [e for e in on if e not in off]

    for c in cores:
        j, S = rank[c], sets[c]
        a = "a%d" % j
        lw, lx = wslot[c] * C, (N + j) * C
        peer = S["peer"][0]
        Ha, Hb = [k for k in world if k not in rank and here(k, c) and topo.die(k) == topo.die(c)
                  and all(topo.may_write(k, d) for d in S["near"])][:2]
        R1, R2f = owners(c, S["far"])[:2]
        R2n = owners(c, S["near"])[1]
        S["order"] = S["far"] + S["near"] + S["plane"] + S["peer"] + [c]
        side = wslot[c] % 2

        off, hi = engines(c, Ha, R1)
        h = _split(off, 2)
        add(c, PLANE, ["qW"], [(Ha, 0, C, "", 0, hi, "rws"), (R2n, 0, C, "", 0, h[0], "rws"), (R1, 0, C, "", 0, h[1], "rws")])
        add(c, CODES, [], [(Hb, 0, C, "", 0, hi, "rwc"), (R2n, 0, C, "", side * C, h[0], "rwc"),
                           (R2f, 0, C, "", side * C, h[1], "rwc")])
        for kind, sm in ((PLANE, "rxs"), (CODES, "rxc")):
            add(c, kind, ["qA1", "qA2"], [(R1, C, 3 * C, "", C, off, sm), (Ha, 3 * C, 5 * C, "", 3 * C, hi, sm)])
        for kind in (PLANE, CODES):
            add(c, kind, ["qB"], [(d, (5 + i) * C, (6 + i) * C, "l", lx, h[i], a) for i, d in enumerate(S["plane"])], srcs=[j])
        for kind in (PLANE, CODES):
            add(c, kind, ["qP"], [(peer, 7 * C, 8 * C, "l", lx, hi, a)], srcs=[j])

        for H, kind, sm in ((Ha, PLANE, "rws"), (Hb, CODES, "rwc")):
            off, hi = engines(H, peer, S["plane"][0])
            h = _split(off, 2)
            add(H, kind, [sm], [(peer, 0, C, "l", lw, hi, a)] + [(d, 0, C, "l", lw, h[i], a) for i, d in enumerate(S["plane"])],
                srcs=[j])
        for kind, sm in ((PLANE, "rxs"), (CODES, "rxc")):
            add(Ha, kind, [sm], [(d, (3 + i) * C, (4 + i) * C, "l", lx, h[i], a) for i, d in enumerate(S["near"])], srcs=[j])

        h = _split(_bits(topo.mask(R1, S["far"][0])), 2)
        add(R1, PLANE, ["rws"], [(d, 0, C, "l", lw, h[i], a) for i, d in enumerate(S["far"])], srcs=[j])
        for kind, sm in ((PLANE, "rxs"), (CODES, "rxc")):
            add(R1, kind, [sm], [(d, (1 + i) * C, (2 + i) * C, "l", lx, h[i], a) for i, d in enumerate(S["far"])], srcs=[j])

        twin = [c2 for c2 in cores if wslot[c2] == wslot[c] ^ 1][0]
        h = _split(_bits(topo.mask(R2n, S["near"][0])), 2)
        add(R2n, PLANE, ["rws"], [(d, 0, C, "l", lw, h[i], a) for i, d in enumerate(S["near"])], srcs=[j])
        add(R2n, CODES, ["rwc"], [(d, 0, 2 * C, "l", (wslot[c] - side) * C, h[i], "b%d" % j) for i, d in enumerate(S["near"])],
            srcs=[j, rank[twin]])
    return {"calls": calls, "expect": expect, "need": need, "sets": sets, "rank": rank, "wslot": wslot}


_CACHE = {}


def rank_program(g, core, T, topo):
    if "plan" not in _CACHE:
        _CACHE["plan"] = _plan(list(T.cores), topo)
    plan = _CACHE["plan"]
    calls, expect = plan["calls"], plan["expect"]
    if core not in calls:
        return
    sem = T.sem

    def view(kind, prefix, a, b):
        if kind == CODES:
            return T[prefix + "q"][:, a:b].bitcast(dt.uint8)
        return T[prefix + "s"][:, a:b]

    def remote_part():
        sent = 0
        for gates, kind, trs in calls[core]:
            for s in gates:
                g.wait_ge(sem[s], expect.get((core, s), 1))
            out = []
            for (dst, a, b, prefix, da, es, sm) in trs:
                rid, pid = topo.addr(dst, core)
                out.append(RemoteDMATransfer(dst_ids=[DstId(rid=rid, pnc=pid)], dma_engine_mask=sum(1 << e for e in es),
                                             remote_sem=sem[sm], src=view(kind, "", a, b),
                                             dst=view(kind, prefix, da, da + b - a)))
                sent += len(es)
            g.remote_dma_fused(out, local_sem=sem.sent)
        g.wait_ge(sem.sent, sent)

    if T.rank_of(core) is None:
        remote_part()
        return

    S = plan["sets"][core]
    rank = plan["rank"]
    order = [rank[d] for d in S["order"]]
    groups = {"A1": (0, 2), "A2": (2, 4), "B": (4, 6), "P": (6, 7), "O": (7, 8)}

    def load(queue, name):
        k0, k1 = groups[name]
        k, n = k0, 0
        while k < k1:
            m = k + 1
            while m < k1 and order[m] == order[m - 1] + 1:
                m += 1
            queue.dma_start(T.xt[:, k * E:m * E], T.x[:, order[k] * E:(order[k] + m - k) * E]).then_inc(sem["l" + name], 16)
            k, n = m, n + 16
        return n

    got = {}
    g.sync.dma_start(T.wt[:, 0:E // 2], T.w[:, 0:E // 2]).then_inc(sem.lW, 16)
    g.scalar.dma_start(T.wt[:, E // 2:E], T.w[:, E // 2:E]).then_inc(sem.lW, 16)
    for i, name in enumerate(GROUPS):
        got[name] = load((g.sync, g.scalar)[i % 2], name)

    v = g.vector
    v.wait_ge(sem.lW, 32)
    v.quantize_mx(T.q[:, 0:C], T.s[:, 0:C], T.wt[:]).then_inc(sem.qW, 1)
    for name in GROUPS:
        k0, k1 = groups[name]
        v.wait_ge(sem["l" + name], got[name])
        v.quantize_mx(T.q[:, (k0 + 1) * C:(k1 + 1) * C], T.s[:, (k0 + 1) * C:(k1 + 1) * C],
                      T.xt[:, k0 * E:k1 * E]).then_inc(sem["q" + name], 1)

    remote_part()

    t = g.tensor
    t.wait_ge(sem.qW, 1)
    t.wait_ge(sem.qO, 1)
    t.matmul_mx(T.ps[:, 0:C], T.q[:, 0:C], T.s[:, 0:C], T.q[:, N * C:(N + 1) * C], T.s[:, N * C:(N + 1) * C], True, False)
    rest = S["peer"] + S["plane"] + S["near"] + S["far"]
    for i, d in enumerate(rest):
        j = rank[d]
        for s in sorted(plan["need"][(core, j)]):
            t.wait_ge(sem[s], expect[(core, s)])
        lw, lx = plan["wslot"][d] * C, (N + j) * C
        mm = t.matmul_mx(T.ps[:, 0:C], T.lq[:, lw:lw + C], T.ls[:, lw:lw + C], T.lq[:, lx:lx + C], T.ls[:, lx:lx + C],
                         False, i == len(rest) - 1)
    mm.then_inc(sem.mm, 1)

    v.wait_ge(sem.mm, 1)
    v.tensor_copy(T.o[:], T.ps[:, 0:C]).then_inc(sem.cp, 1)
    g.sync.wait_ge(sem.cp, 1)
    g.sync.dma_start(T.y[:], T.o[:]).then_inc(sem.st, 16)
    g.sync.wait_ge(sem.st, 16)
